import numpy as np
import ml_dtypes


def mxq(x, axis, fmt="e4m3"):
    dtype, down = {"e4m3": (ml_dtypes.float8_e4m3fn, 7), "e5m2": (ml_dtypes.float8_e5m2, 14)}[fmt]
    v = np.moveaxis(np.asarray(x, np.float32).astype(ml_dtypes.bfloat16).astype(np.float64), axis, -1)
    blocks = v.reshape(v.shape[:-1] + (-1, 32))
    amax = np.abs(blocks).max(-1, keepdims=True)
    byte = np.maximum(np.where(amax > 0, np.frexp(amax)[1] - 1 + 127, 0) - down, 1)
    scale = np.exp2(byte - 127.0)
    codes = (blocks / scale).astype(np.float32).astype(dtype).astype(np.float64)
    return np.moveaxis((codes * scale).reshape(v.shape), -1, axis)


WIDE = False


def mx_kscale(k):
    if not WIDE:
        return np.ones(k)
    levels = np.array([10, -10, 5, -5, 0])
    if k % 512:
        return np.exp2(np.random.permutation(np.resize(levels, k // 32))).repeat(32)
    a = np.empty((k // 512, 16))
    for p in range(k // 512):
        a[p, :8] = np.random.permutation(np.resize(levels, 8))
        for g in range(8):
            far = levels[np.abs(levels - a[p, g]) >= 10]
            a[p, g + 8] = far[np.random.randint(len(far))]
    return np.exp2(a.ravel()).repeat(32)


def f64(x):
    return np.asarray(x).astype(np.float64)


def striped(idx):
    return np.tile(idx.reshape(-1, 16).T, (8, 1)).astype(np.uint16)


def unstriped(offs):
    return offs[:16].T.reshape(-1).astype(np.int64)


E2M1 = np.array([0.0, 0.5, 1.0, 1.5, 2.0, 3.0, 4.0, 6.0, -0.0, -0.5, -1.0, -1.5, -2.0, -3.0, -4.0, -6.0])


def pack_weight(w, fmt):
    k, n = w.shape
    w = f64(np.asarray(w, np.float32).astype(ml_dtypes.bfloat16)).reshape(k // 32, 32, n)
    amax = np.abs(w).max(1)
    if fmt == "e4m3":
        byte = np.frexp(amax)[1] - 1 + 127 - 7
    else:
        mant, ex = np.frexp(amax / 6.0)
        byte = np.where(mant > 0.5, ex, ex - 1) + 127
    byte = np.clip(np.where(amax > 0, byte, 1), 1, 254)
    scaled = (w * np.exp2(127.0 - byte)[:, None, :]).reshape(k, n).astype(np.float32)
    by_word = np.ascontiguousarray(scaled.reshape(k // 512, 128, 4, n).transpose(0, 1, 3, 2))
    if fmt == "e4m3":
        words = by_word.astype(ml_dtypes.float8_e4m3fn).view(np.uint8)
    else:
        c = by_word.astype(ml_dtypes.float4_e2m1fn).view(np.uint8) & 0xF
        words = (c[..., 0::2] | (c[..., 1::2] << 4)).reshape(k // 512, 128, 2 * n)
    return np.ascontiguousarray(words), np.ascontiguousarray(byte.astype(np.uint8).reshape(k // 512, 16, n))


def unpack_weight(words, scales, fmt):
    g, _, n = scales.shape
    words = np.ascontiguousarray(words).reshape(g, 128, n, -1)
    if fmt == "e4m3":
        vals = words.view(ml_dtypes.float8_e4m3fn).astype(np.float64)
    else:
        nib = np.empty((g, 128, n, 4), np.uint8)
        nib[..., 0::2] = words & 0xF
        nib[..., 1::2] = words >> 4
        vals = E2M1[nib]
    vals = vals * np.repeat(np.exp2(scales.astype(np.float64) - 127.0), 8, axis=1)[..., None]
    return vals.transpose(0, 1, 3, 2).reshape(g * 512, n)


def silu(v):
    return v / (1.0 + np.exp(-np.maximum(v, -700.0)))


K, T, E, C, H, N = 1024, 1024, 6, 128, 512, 384


def by_expert(wq, xq):
    return np.concatenate([wq[e].T @ xq[:, e * C:(e + 1) * C] for e in range(E)], axis=1)


def setup_inputs():
    n = np.random.standard_normal
    s = mx_kscale(K)[:, None]
    u = mx_kscale(H)
    w1 = [pack_weight(m, "e2m1") for m in n((E, K, H)) / np.sqrt(K) / s[None] * u[None, None, :]]
    w2 = [pack_weight(m, "e2m1") for m in n((E, H, N)) / np.sqrt(H) / u[None, :, None]]
    return {
        "xT": (n((K, T)) * s).astype(np.float32),
        "w1_words": np.stack([m[0] for m in w1]),
        "w1_scales": np.stack([m[1] for m in w1]),
        "w2_words": np.stack([m[0] for m in w2]),
        "w2_scales": np.stack([m[1] for m in w2]),
        "gate": np.tile(np.random.uniform(0.2, 1.0, E * C), (K, 1)).astype(np.float32),
        "offs": striped(np.random.permutation(T)[:E * C]),
    }


def reference(xT, w1_words, w1_scales, w2_words, w2_scales, gate, offs):
    idx = unstriped(offs)
    w1 = np.stack([unpack_weight(w1_words[e], w1_scales[e], "e2m1") for e in range(E)])
    w2 = np.stack([unpack_weight(w2_words[e], w2_scales[e], "e2m1") for e in range(E)])
    xq = mxq(f64(gate) * f64(xT)[:, idx], 0, "e4m3")
    h = silu(by_expert(w1, xq))
    y = by_expert(w2, mxq(h, 0, "e4m3"))
    out = np.zeros((N, T))
    out[:, idx] = y
    return out

@@ -1,0 +1,170 @@
+from contextlib import ExitStack
+
+import concourse.mybir as mybir
+from concourse.masks import make_identity
+
+K, T, E, C, H, N = 1024, 1024, 6, 128, 512, 384
+SLOTS = E * C
+FLOPS = 2 * SLOTS * (K * H + H * N)
+BYTES = 4 * K * T + E * (K * H + H * N) // 2 + E * (K * H + H * N) // 32 + 4 * SLOTS + 2 * 128 * SLOTS // 16 + 4 * N * T
+
+F32 = mybir.dt.float32
+BF16 = mybir.dt.bfloat16
+I32 = mybir.dt.int32
+U32 = mybir.dt.uint32
+U16 = mybir.dt.uint16
+U8 = mybir.dt.uint8
+FP8X4 = mybir.dt.float8_e4m3fn_x4
+FP4X4 = mybir.dt.float4_e2m1fn_x4
+SILU = mybir.ActivationFunctionType.Silu
+MULT = mybir.AluOpType.mult
+
+P = 128
+PACK = 4
+PASSES = K // (P * PACK)
+N_TILES = N // P
+GROUPS = ((0, 2), (2, 4), (4, 6))
+
+
+def tile_moe_pre_mlp_silu_kernel(tc, xT, w1_words, w1_scales, w2_words, w2_scales, gate, offs, out):
+    nc = tc.nc
+    with ExitStack() as ctx:
+        held = ctx.enter_context(tc.tile_pool(name="held", bufs=1))
+        a_psum = ctx.enter_context(tc.psum_pool(name="a_psum", bufs=3))
+        turn_psum = ctx.enter_context(tc.psum_pool(name="turn_psum", bufs=2))
+        y_psum = ctx.enter_context(tc.psum_pool(name="y_psum", bufs=3))
+
+        def sbuf(name, shape, dtype):
+            return held.tile(shape, dtype, name=name, align_bytes=64)
+
+        offsets = held.tile([P, SLOTS // 16], U16, name="offsets")
+        nc.sync.dma_start(offsets[:], offs)
+
+        def offsets_of(first, last):
+            return offsets[:, first * C // 16 : last * C // 16]
+
+        plane1 = sbuf("plane1", [P, E * PASSES, H], U8)
+        plane2 = sbuf("plane2", [P, E, N], U8)
+        result = [sbuf(f"result{j}", [P, T], F32) for j in range(N_TILES)]
+        nc.vector.memset(result[0][:], 0.0)
+        nc.vector.memset(plane1[:].bitcast(I32), 0)
+        nc.vector.memset(plane2[:].bitcast(I32), 0)
+        nc.scalar.activation(result[1][:], result[0][:], SILU)
+        nc.scalar.copy(result[2][:], result[0][:])
+        identity = sbuf("identity", [P, P], F32)
+        make_identity(nc, identity[:])
+
+        x_rows = xT.rearrange("(s p t) n -> s t p n", p=P, t=PACK)
+        window = [[sbuf(f"window{s}{t}", [P, T], F32) for t in range(PACK)] for s in range(PASSES)]
+        gates = [sbuf(f"gates{g}", [P, (hi - lo) * C], F32) for g, (lo, hi) in enumerate(GROUPS)]
+        words1 = [sbuf(f"words1_{g}", [P, (hi - lo) * PASSES, 2 * H], U8) for g, (lo, hi) in enumerate(GROUPS)]
+        words2 = [sbuf(f"words2_{g}", [P, hi - lo, 2 * N], U8) for g, (lo, hi) in enumerate(GROUPS)]
+
+        def load_gates(g):
+            lo, hi = GROUPS[g]
+            nc.sync.dma_start(gates[g][:], gate[0:P, lo * C : hi * C])
+
+        def load_words1(g):
+            lo, hi = GROUPS[g]
+            nc.sync.dma_start(words1[g][:], w1_words[lo:hi].rearrange("e s p b -> p (e s) b"))
+
+        def load_words2(g):
+            lo, hi = GROUPS[g]
+            nc.sync.dma_start(words2[g][:], w2_words[lo:hi].rearrange("e s p b -> p (e s) b"))
+
+        def load_plane(plane, scales):
+            rows = scales.rearrange("e s (q r) i -> r q (e s) i", r=4)
+            for r in range(4):
+                nc.sync.dma_start(plane[:].bitcast(I32)[r:P:32], rows[r].bitcast(I32))
+
+        load_gates(0)
+        nc.sync.dma_start(window[0][0][:], x_rows[0, 0])
+        for g in range(1, len(GROUPS)):
+            load_gates(g)
+        for s in range(PASSES):
+            for t in range(PACK):
+                if (s, t) != (0, 0):
+                    nc.sync.dma_start(window[s][t][:], x_rows[s, t])
+        load_plane(plane1, w1_scales)
+        load_words1(0)
+        load_plane(plane2, w2_scales)
+        load_words2(0)
+        for g in range(1, len(GROUPS)):
+            load_words1(g)
+            load_words2(g)
+
+        y = [sbuf(f"y{j}", [P, SLOTS], F32) for j in range(N_TILES)]
+
+        for g, (lo, hi) in enumerate(GROUPS):
+            width = (hi - lo) * C
+            x_codes, x_scales = [], []
+            for s in range(PASSES):
+                gathered = sbuf(f"gathered{g}{s}", [P, PACK, width], F32)
+                for t in range(PACK):
+                    nc.vector.tensor_tensor(
+                        gathered[:, t, :], window[s][t][:].indirect(offsets_of(lo, hi)), gates[g][:], MULT
+                    )
+                x_bf = sbuf(f"x_bf{g}{s}", [P, width, PACK], BF16)
+                nc.scalar.copy(
+                    x_bf[:].rearrange("p (c i) t -> p c t i", i=4),
+                    gathered[:].rearrange("p t (c i) -> p c t i", i=4),
+                )
+                codes = sbuf(f"x_codes{g}{s}", [P, width], U32)
+                scales = sbuf(f"x_scales{g}{s}", [P, width], U8)
+                nc.vector.quantize_mx(
+                    out=codes[:].bitcast(FP8X4), scales=scales[:], in_=x_bf[:].rearrange("p n t -> p (n t)")
+                )
+                x_codes.append(codes)
+                x_scales.append(scales)
+
+            turned = turn_psum.tile([P, hi - lo, 2, C], F32, name="turned")
+            for e in range(lo, hi):
+                slots = slice((e - lo) * C, (e - lo + 1) * C)
+                a = a_psum.tile([C, H], F32, name="a")
+                for s in range(PASSES):
+                    nc.tensor.matmul_mx(
+                        out=a[:],
+                        lhsT=x_codes[s][:, slots].bitcast(FP8X4),
+                        lhsT_scale=x_scales[s][:, slots],
+                        rhs=words1[g][:, (e - lo) * PASSES + s, :].bitcast(FP4X4),
+                        rhs_scale=plane1[:, e * PASSES + s, :],
+                        start=(s == 0),
+                        stop=(s == PASSES - 1),
+                    )
+                h_rows = sbuf(f"h_rows{e}", [C, H], BF16)
+                nc.scalar.activation(
+                    h_rows[:].rearrange("m (u p d) -> m u p d", u=2, d=2),
+                    a[:].rearrange("m (p u d) -> m u p d", u=2, d=2),
+                    SILU,
+                )
+                pairs = h_rows[:].bitcast(F32)
+                for u in range(2):
+                    nc.tensor.transpose(turned[:, e - lo, u, :], pairs[:, u * P : (u + 1) * P], identity[:])
+            h_bf = sbuf(f"h_bf{g}", [P, width * PACK], BF16)
+            nc.scalar.copy(
+                h_bf[:].bitcast(F32).rearrange("p (e c u) -> p e c u", c=C, u=2),
+                turned[:].rearrange("p e u c -> p e c u"),
+            )
+            h_codes = sbuf(f"h_codes{g}", [P, width], U32)
+            h_scales = sbuf(f"h_scales{g}", [P, width], U8)
+            nc.vector.quantize_mx(out=h_codes[:].bitcast(FP8X4), scales=h_scales[:], in_=h_bf[:])
+
+            for j in range(N_TILES):
+                y_bank = y_psum.tile([P, width], F32, name="y_bank")
+                for e in range(lo, hi):
+                    slots = slice((e - lo) * C, (e - lo + 1) * C)
+                    nc.tensor.matmul_mx(
+                        out=y_bank[:, slots],
+                        lhsT=words2[g][:, e - lo, 2 * P * j : 2 * P * (j + 1)].bitcast(FP4X4),
+                        lhsT_scale=plane2[:, e, P * j : P * (j + 1)],
+                        rhs=h_codes[:, slots].bitcast(FP8X4),
+                        rhs_scale=h_scales[:, slots],
+                        start=True,
+                        stop=True,
+                    )
+                nc.scalar.copy(y[j][:, lo * C : hi * C], y_bank[:])
+
+        for j in range(N_TILES):
+            for lo, hi in GROUPS:
+                nc.vector.tensor_copy(result[j][:].indirect(offsets_of(lo, hi)), y[j][:, lo * C : hi * C])
+            nc.sync.dma_start(out[j * P : (j + 1) * P, :], result[j][:])

@@ -23,32 +23,34 @@ P = 128
 PACK = 4
 PASSES = K // (P * PACK)
 N_TILES = N // P
-GROUPS = ((0, 2), (2, 4), (4, 6))
+PAIR = 2 * C
+A, B, D = 0, 1, 2
 
 
 def tile_moe_pre_mlp_silu_kernel(tc, xT, w1_words, w1_scales, w2_words, w2_scales, gate, offs, out):
     nc = tc.nc
     with ExitStack() as ctx:
         held = ctx.enter_context(tc.tile_pool(name="held", bufs=1))
-        a_psum = ctx.enter_context(tc.psum_pool(name="a_psum", bufs=3))
-        turn_psum = ctx.enter_context(tc.psum_pool(name="turn_psum", bufs=2))
-        y_psum = ctx.enter_context(tc.psum_pool(name="y_psum", bufs=3))
+        psum = ctx.enter_context(tc.psum_pool(name="psum", bufs=1))
 
-        def sbuf(name, shape, dtype):
-            return held.tile(shape, dtype, name=name, align_bytes=64)
+        def sbuf(name, shape, dtype, tag=None):
+            return held.tile(shape, dtype, name=name, tag=tag or name, align_bytes=64)
+
+        def bank(name, shape, tag):
+            return psum.tile(shape, F32, name=name, tag=tag)
 
         offsets = held.tile([P, SLOTS // 16], U16, name="offsets")
         nc.sync.dma_start(offsets[:], offs)
 
         def offsets_of(first, last):
-            return offsets[:, first * C // 16 : last * C // 16]
+            return offsets[:, first * PAIR // 16 : last * PAIR // 16]
 
         plane1 = sbuf("plane1", [P, E * PASSES, H], U8)
         plane2 = sbuf("plane2", [P, E, N], U8)
         result = [sbuf(f"result{j}", [P, T], F32) for j in range(N_TILES)]
         nc.vector.memset(result[0][:], 0.0)
-        nc.vector.memset(plane1[:].bitcast(I32), 0)
-        nc.vector.memset(plane2[:].bitcast(I32), 0)
+        nc.gpsimd.memset(plane1[:].bitcast(I32), 0)
+        nc.gpsimd.memset(plane2[:].bitcast(I32), 0)
         nc.scalar.activation(result[1][:], result[0][:], SILU)
         nc.scalar.copy(result[2][:], result[0][:])
         identity = sbuf("identity", [P, P], F32)
@@ -56,82 +58,77 @@ def tile_moe_pre_mlp_silu_kernel(tc, xT, w1_words, w1_scales, w2_words, w2_scale
 
         x_rows = xT.rearrange("(s p t) n -> s t p n", p=P, t=PACK)
         window = [[sbuf(f"window{s}{t}", [P, T], F32) for t in range(PACK)] for s in range(PASSES)]
-        gates = [sbuf(f"gates{g}", [P, (hi - lo) * C], F32) for g, (lo, hi) in enumerate(GROUPS)]
-        words1 = [sbuf(f"words1_{g}", [P, (hi - lo) * PASSES, 2 * H], U8) for g, (lo, hi) in enumerate(GROUPS)]
-        words2 = [sbuf(f"words2_{g}", [P, hi - lo, 2 * N], U8) for g, (lo, hi) in enumerate(GROUPS)]
+        words1 = [sbuf(f"words1_{g}", [P, 2 * PASSES, 2 * H], U8) for g in (A, B, D)]
+        words2 = [sbuf(f"words2_{g}", [P, 2, 2 * N], U8) for g in (A, B, D)]
 
-        def load_gates(g):
-            lo, hi = GROUPS[g]
-            nc.sync.dma_start(gates[g][:], gate[0:P, lo * C : hi * C])
+        shared0 = sbuf("shared0", [P, 5 * PAIR], F32)
+        shared1 = sbuf("shared1", [P, 4 * PAIR], F32)
+        gates_ab = shared0[:, 0 : 2 * PAIR]
+        gathered_d = [
+            shared0[:, PAIR : 5 * PAIR].rearrange("p (t n) -> p t n", t=PACK),
+            shared1[:].rearrange("p (t n) -> p t n", t=PACK),
+        ]
+        x_bf_a1 = shared0[:, 5 * PAIR // 2 : 9 * PAIR // 2].bitcast(BF16)
+        x_bf_b1 = shared1[:, 0 : 2 * PAIR].bitcast(BF16)
+        h_bf_a = shared1[:, 2 * PAIR : 4 * PAIR].bitcast(BF16)
+        gates_d = sbuf("gates_d", [P, PAIR], F32)
 
-        def load_words1(g):
-            lo, hi = GROUPS[g]
-            nc.sync.dma_start(words1[g][:], w1_words[lo:hi].rearrange("e s p b -> p (e s) b"))
+        def load_words(g):
+            nc.sync.dma_start(words1[g][:], w1_words[2 * g : 2 * g + 2].rearrange("e s p b -> p (e s) b"))
 
         def load_words2(g):
-            lo, hi = GROUPS[g]
-            nc.sync.dma_start(words2[g][:], w2_words[lo:hi].rearrange("e s p b -> p (e s) b"))
+            nc.sync.dma_start(words2[g][:], w2_words[2 * g : 2 * g + 2].rearrange("e s p b -> p (e s) b"))
 
         def load_plane(plane, scales):
             rows = scales.rearrange("e s (q r) i -> r q (e s) i", r=4)
             for r in range(4):
                 nc.sync.dma_start(plane[:].bitcast(I32)[r:P:32], rows[r].bitcast(I32))
 
-        load_gates(0)
-        nc.sync.dma_start(window[0][0][:], x_rows[0, 0])
-        for g in range(1, len(GROUPS)):
-            load_gates(g)
+        nc.sync.dma_start(gates_ab, gate[0:P, 0 : 2 * PAIR])
         for s in range(PASSES):
             for t in range(PACK):
-                if (s, t) != (0, 0):
-                    nc.sync.dma_start(window[s][t][:], x_rows[s, t])
+                nc.sync.dma_start(window[s][t][:], x_rows[s, t])
+        nc.sync.dma_start(gates_d[:], gate[0:P, 2 * PAIR : 3 * PAIR])
         load_plane(plane1, w1_scales)
-        load_words1(0)
+        load_words(A)
+        load_words(B)
         load_plane(plane2, w2_scales)
-        load_words2(0)
-        for g in range(1, len(GROUPS)):
-            load_words1(g)
-            load_words2(g)
+        load_words2(A)
+        load_words2(B)
+        load_words(D)
+        load_words2(D)
 
-        y = [sbuf(f"y{j}", [P, SLOTS], F32) for j in range(N_TILES)]
+        def gather(dst, s, t, first, last, gates):
+            nc.vector.tensor_tensor(dst, window[s][t][:].indirect(offsets_of(first, last)), gates, MULT)
 
-        for g, (lo, hi) in enumerate(GROUPS):
-            width = (hi - lo) * C
-            x_codes, x_scales = [], []
-            for s in range(PASSES):
-                gathered = sbuf(f"gathered{g}{s}", [P, PACK, width], F32)
-                for t in range(PACK):
-                    nc.vector.tensor_tensor(
-                        gathered[:, t, :], window[s][t][:].indirect(offsets_of(lo, hi)), gates[g][:], MULT
-                    )
-                x_bf = sbuf(f"x_bf{g}{s}", [P, width, PACK], BF16)
-                nc.scalar.copy(
-                    x_bf[:].rearrange("p (c i) t -> p c t i", i=4),
-                    gathered[:].rearrange("p t (c i) -> p c t i", i=4),
-                )
-                codes = sbuf(f"x_codes{g}{s}", [P, width], U32)
-                scales = sbuf(f"x_scales{g}{s}", [P, width], U8)
-                nc.vector.quantize_mx(
-                    out=codes[:].bitcast(FP8X4), scales=scales[:], in_=x_bf[:].rearrange("p n t -> p (n t)")
-                )
-                x_codes.append(codes)
-                x_scales.append(scales)
+        def interleave(dst, src):
+            nc.scalar.copy(
+                dst.rearrange("p (c i t) -> p c t i", i=4, t=PACK),
+                src.rearrange("p t (c i) -> p c t i", i=4),
+            )
 
-            turned = turn_psum.tile([P, hi - lo, 2, C], F32, name="turned")
-            for e in range(lo, hi):
-                slots = slice((e - lo) * C, (e - lo + 1) * C)
-                a = a_psum.tile([C, H], F32, name="a")
-                for s in range(PASSES):
+        def quantize(name, src, words, tag=None):
+            codes = sbuf(f"{name}_codes", [P, words], U32, tag)
+            scales = sbuf(f"{name}_scales", [P, words], U8)
+            nc.vector.quantize_mx(out=codes[:].bitcast(FP8X4), scales=scales[:], in_=src)
+            return codes, scales
+
+        def first_layer(g, x_passes, h_bf, turned_tag, tag=None):
+            turned = bank(f"turned{g}", [P, 2, 2, C], turned_tag)
+            for i in range(2):
+                a = bank(f"a{g}{i}", [C, H], f"a{i}")
+                for s, (codes, scales, first) in enumerate(x_passes):
+                    slots = slice(first + i * C, first + (i + 1) * C)
                     nc.tensor.matmul_mx(
                         out=a[:],
-                        lhsT=x_codes[s][:, slots].bitcast(FP8X4),
-                        lhsT_scale=x_scales[s][:, slots],
-                        rhs=words1[g][:, (e - lo) * PASSES + s, :].bitcast(FP4X4),
-                        rhs_scale=plane1[:, e * PASSES + s, :],
+                        lhsT=codes[:, slots].bitcast(FP8X4),
+                        lhsT_scale=scales[:, slots],
+                        rhs=words1[g][:, i * PASSES + s, :].bitcast(FP4X4),
+                        rhs_scale=plane1[:, (2 * g + i) * PASSES + s, :],
                         start=(s == 0),
                         stop=(s == PASSES - 1),
                     )
-                h_rows = sbuf(f"h_rows{e}", [C, H], BF16)
+                h_rows = sbuf(f"h_rows{g}{i}", [C, H], BF16)
                 nc.scalar.activation(
                     h_rows[:].rearrange("m (u p d) -> m u p d", u=2, d=2),
                     a[:].rearrange("m (p u d) -> m u p d", u=2, d=2),
@@ -139,32 +136,83 @@ def tile_moe_pre_mlp_silu_kernel(tc, xT, w1_words, w1_scales, w2_words, w2_scale
                 )
                 pairs = h_rows[:].bitcast(F32)
                 for u in range(2):
-                    nc.tensor.transpose(turned[:, e - lo, u, :], pairs[:, u * P : (u + 1) * P], identity[:])
-            h_bf = sbuf(f"h_bf{g}", [P, width * PACK], BF16)
+                    nc.tensor.transpose(turned[:, i, u, :], pairs[:, u * P : (u + 1) * P], identity[:])
             nc.scalar.copy(
-                h_bf[:].bitcast(F32).rearrange("p (e c u) -> p e c u", c=C, u=2),
+                h_bf.bitcast(F32).rearrange("p (e c u) -> p e c u", c=C, u=2),
                 turned[:].rearrange("p e u c -> p e c u"),
             )
-            h_codes = sbuf(f"h_codes{g}", [P, width], U32)
-            h_scales = sbuf(f"h_scales{g}", [P, width], U8)
-            nc.vector.quantize_mx(out=h_codes[:].bitcast(FP8X4), scales=h_scales[:], in_=h_bf[:])
+            return quantize(f"h{g}", h_bf, PAIR, tag)
 
-            for j in range(N_TILES):
-                y_bank = y_psum.tile([P, width], F32, name="y_bank")
-                for e in range(lo, hi):
-                    slots = slice((e - lo) * C, (e - lo + 1) * C)
-                    nc.tensor.matmul_mx(
-                        out=y_bank[:, slots],
-                        lhsT=words2[g][:, e - lo, 2 * P * j : 2 * P * (j + 1)].bitcast(FP4X4),
-                        lhsT_scale=plane2[:, e, P * j : P * (j + 1)],
-                        rhs=h_codes[:, slots].bitcast(FP8X4),
-                        rhs_scale=h_scales[:, slots],
-                        start=True,
-                        stop=True,
-                    )
-                nc.scalar.copy(y[j][:, lo * C : hi * C], y_bank[:])
+        def second_layer(g, j, h, bank_tag):
+            codes, scales = h
+            y_bank = bank(f"y_bank{g}{j}", [P, PAIR], bank_tag)
+            for i in range(2):
+                slots = slice(i * C, (i + 1) * C)
+                nc.tensor.matmul_mx(
+                    out=y_bank[:, slots],
+                    lhsT=words2[g][:, i, 2 * P * j : 2 * P * (j + 1)].bitcast(FP4X4),
+                    lhsT_scale=plane2[:, 2 * g + i, P * j : P * (j + 1)],
+                    rhs=codes[:, slots].bitcast(FP8X4),
+                    rhs_scale=scales[:, slots],
+                    start=True,
+                    stop=True,
+                )
+            return y_bank
 
+        def scatter(g, j, y):
+            nc.vector.tensor_copy(result[j][:].indirect(offsets_of(g, g + 1)), y)
+
+        gathered_ab = [sbuf(f"gathered_ab{s}", [P, PACK, 2 * PAIR], F32) for s in range(PASSES)]
+        for t in range(PACK):
+            gather(gathered_ab[0][:, t, :], 0, t, A, D, gates_ab)
+        x_bf_ab0 = sbuf("x_bf_ab0", [P, 2 * PAIR * PACK], BF16)
+        interleave(x_bf_ab0[:], gathered_ab[0][:])
+        x_ab0 = quantize("x_ab0", x_bf_ab0[:], 2 * PAIR)
+        for t in range(PACK - 1):
+            gather(gathered_ab[1][:, t, :], 1, t, A, D, gates_ab)
+        for g in (A, B):
+            cols = slice(g * PAIR, (g + 1) * PAIR)
+            gather(gathered_ab[1][:, PACK - 1, cols], 1, PACK - 1, g, g + 1, gates_ab[:, cols])
+
+        interleave(x_bf_a1, gathered_ab[1][:, :, 0:PAIR])
+        x_a1 = quantize("x_a1", x_bf_a1, PAIR)
+        interleave(x_bf_b1, gathered_ab[1][:, :, PAIR : 2 * PAIR])
+        x_b1 = quantize("x_b1", x_bf_b1, PAIR)
+
+        h_a = first_layer(A, [(*x_ab0, 0), (*x_a1, 0)], h_bf_a, "bank2", "h_codes_a")
+        banks_a = [second_layer(A, j, h_a, tag) for j, tag in enumerate(("bank5", "bank7", "bank6"))]
+        y_early = sbuf("y_early", [P, 2, PAIR], F32)
+        for j in range(2):
+            nc.scalar.copy(y_early[:, j, :], banks_a[j][:])
+
+        h_bf_b = sbuf("h_bf_b", [P, PAIR * PACK], BF16)
+        h_b = first_layer(B, [(*x_ab0, PAIR), (*x_b1, 0)], h_bf_b[:], "bank3")
+
+        x_bf_d = sbuf("x_bf_d", [P, PASSES, PAIR * PACK], BF16, "h_codes_a")
+        for s in range(PASSES):
+            for t in range(PACK):
+                gather(gathered_d[s][:, t, :], s, t, D, D + 1, gates_d[:])
+            interleave(x_bf_d[:, s, :], gathered_d[s])
+        x_d = quantize("x_d", x_bf_d[:].rearrange("p s n -> p (s n)"), PASSES * PAIR)
+
+        y_middle = sbuf("y_middle", [P, 3, PAIR], F32, "shared1")
+        nc.scalar.copy(y_middle[:, 0, :], banks_a[2][:])
+        for j, tag in enumerate(("bank2", "bank5")):
+            nc.scalar.copy(y_middle[:, 1 + j, :], second_layer(B, j, h_b, tag)[:])
+
+        h_bf_d = sbuf("h_bf_d", [P, PAIR * PACK], BF16)
+        h_d = first_layer(D, [(*x_d, 0), (*x_d, PAIR)], h_bf_d[:], "bank4")
+        y_late = sbuf("y_late", [P, 4, PAIR], F32)
+        nc.scalar.copy(y_late[:, 0, :], second_layer(B, 2, h_b, "bank4")[:])
+        for j, tag in enumerate(("bank3", "bank7", "bank6")):
+            nc.scalar.copy(y_late[:, 1 + j, :], second_layer(D, j, h_d, tag)[:])
+
+        scatter(A, 0, y_early[:, 0, :])
+        scatter(A, 1, y_early[:, 1, :])
+        scatter(A, 2, y_middle[:, 0, :])
+        scatter(B, 0, y_middle[:, 1, :])
+        scatter(B, 1, y_middle[:, 2, :])
+        scatter(B, 2, y_late[:, 0, :])
         for j in range(N_TILES):
-            for lo, hi in GROUPS:
-                nc.vector.tensor_copy(result[j][:].indirect(offsets_of(lo, hi)), y[j][:, lo * C : hi * C])
+            scatter(D, j, y_late[:, 1 + j, :])
             nc.sync.dma_start(out[j * P : (j + 1) * P, :], result[j][:])

@@ -24,7 +24,7 @@ PACK = 4
 PASSES = K // (P * PACK)
 N_TILES = N // P
 PAIR = 2 * C
-A, B, D = 0, 1, 2
+B, D, A = 0, 1, 2
 
 
 def tile_moe_pre_mlp_silu_kernel(tc, xT, w1_words, w1_scales, w2_words, w2_scales, gate, offs, out):
@@ -40,16 +40,18 @@ def tile_moe_pre_mlp_silu_kernel(tc, xT, w1_words, w1_scales, w2_words, w2_scale
             return psum.tile(shape, F32, name=name, tag=tag)
 
         offsets = held.tile([P, SLOTS // 16], U16, name="offsets")
-        nc.sync.dma_start(offsets[:], offs)
 
         def offsets_of(first, last):
             return offsets[:, first * PAIR // 16 : last * PAIR // 16]
 
-        plane1 = sbuf("plane1", [P, E * PASSES, H], U8)
+        plane1_bd = sbuf("plane1_bd", [P, 4 * PASSES, H], U8)
+        plane1_a = sbuf("plane1_a", [P, 2 * PASSES, H], U8)
+        plane1 = [plane1_bd[:, 0 : 2 * PASSES], plane1_bd[:, 2 * PASSES : 4 * PASSES], plane1_a[:]]
         plane2 = sbuf("plane2", [P, E, N], U8)
         result = [sbuf(f"result{j}", [P, T], F32) for j in range(N_TILES)]
-        nc.vector.memset(result[0][:], 0.0)
-        nc.gpsimd.memset(plane1[:].bitcast(I32), 0)
+        nc.gpsimd.memset(result[0][:], 0.0)
+        nc.gpsimd.memset(plane1_a[:].bitcast(I32), 0)
+        nc.gpsimd.memset(plane1_bd[:].bitcast(I32), 0)
         nc.gpsimd.memset(plane2[:].bitcast(I32), 0)
         nc.scalar.activation(result[1][:], result[0][:], SILU)
         nc.scalar.copy(result[2][:], result[0][:])
@@ -58,48 +60,51 @@ def tile_moe_pre_mlp_silu_kernel(tc, xT, w1_words, w1_scales, w2_words, w2_scale
 
         x_rows = xT.rearrange("(s p t) n -> s t p n", p=P, t=PACK)
         window = [[sbuf(f"window{s}{t}", [P, T], F32) for t in range(PACK)] for s in range(PASSES)]
-        words1 = [sbuf(f"words1_{g}", [P, 2 * PASSES, 2 * H], U8) for g in (A, B, D)]
-        words2 = [sbuf(f"words2_{g}", [P, 2, 2 * N], U8) for g in (A, B, D)]
+        words1 = [sbuf(f"words1_{g}", [P, 2 * PASSES, 2 * H], U8) for g in range(3)]
+        words2 = [sbuf(f"words2_{g}", [P, 2, 2 * N], U8) for g in range(3)]
 
-        shared0 = sbuf("shared0", [P, 5 * PAIR], F32)
-        shared1 = sbuf("shared1", [P, 4 * PAIR], F32)
-        gates_ab = shared0[:, 0 : 2 * PAIR]
-        gathered_d = [
-            shared0[:, PAIR : 5 * PAIR].rearrange("p (t n) -> p t n", t=PACK),
-            shared1[:].rearrange("p (t n) -> p t n", t=PACK),
-        ]
-        x_bf_a1 = shared0[:, 5 * PAIR // 2 : 9 * PAIR // 2].bitcast(BF16)
-        x_bf_b1 = shared1[:, 0 : 2 * PAIR].bitcast(BF16)
-        h_bf_a = shared1[:, 2 * PAIR : 4 * PAIR].bitcast(BF16)
-        gates_d = sbuf("gates_d", [P, PAIR], F32)
+        shared = sbuf("shared", [P, 11 * PAIR], F32)
+        gates = shared[:, 0 : 3 * PAIR]
+        gathered_bd1 = shared[:, 2 * PAIR : 10 * PAIR].rearrange("p (t n) -> p t n", t=PACK)
+        x_bf_a1 = shared[:, 5 * PAIR : 7 * PAIR].bitcast(BF16)
+        h_bf_a = shared[:, 9 * PAIR : 11 * PAIR].bitcast(BF16)
 
-        def load_words(g):
-            nc.sync.dma_start(words1[g][:], w1_words[2 * g : 2 * g + 2].rearrange("e s p b -> p (e s) b"))
+        def load_window(s, t):
+            nc.sync.dma_start(window[s][t][:], x_rows[s, t])
 
-        def load_words2(g):
-            nc.sync.dma_start(words2[g][:], w2_words[2 * g : 2 * g + 2].rearrange("e s p b -> p (e s) b"))
+        def load_words(tiles, words, g):
+            nc.sync.dma_start(tiles[g][:], words[2 * g : 2 * g + 2].rearrange("e s p b -> p (e s) b"))
 
         def load_plane(plane, scales):
             rows = scales.rearrange("e s (q r) i -> r q (e s) i", r=4)
             for r in range(4):
                 nc.sync.dma_start(plane[:].bitcast(I32)[r:P:32], rows[r].bitcast(I32))
 
-        nc.sync.dma_start(gates_ab, gate[0:P, 0 : 2 * PAIR])
+        load_window(0, 0)
+        nc.sync.dma_start(gates[:, 0:PAIR], gate[0:P, 0:PAIR])
+        nc.sync.dma_start(offsets[:], offs)
+        nc.sync.dma_start(gates[:, PAIR:SLOTS], gate[0:P, PAIR:SLOTS])
         for s in range(PASSES):
             for t in range(PACK):
-                nc.sync.dma_start(window[s][t][:], x_rows[s, t])
-        nc.sync.dma_start(gates_d[:], gate[0:P, 2 * PAIR : 3 * PAIR])
-        load_plane(plane1, w1_scales)
-        load_words(A)
-        load_words(B)
+                if (s, t) != (0, 0):
+                    load_window(s, t)
+        load_plane(plane1_a, w1_scales[2 * A : 2 * A + 2])
+        load_words(words1, w1_words, A)
         load_plane(plane2, w2_scales)
-        load_words2(A)
-        load_words2(B)
-        load_words(D)
-        load_words2(D)
+        load_words(words2, w2_words, A)
+        load_plane(plane1_bd, w1_scales[2 * B : 2 * D + 2])
+        load_words(words1, w1_words, B)
+        load_words(words2, w2_words, B)
+        load_words(words1, w1_words, D)
+        load_words(words2, w2_words, D)
 
-        def gather(dst, s, t, first, last, gates):
-            nc.vector.tensor_tensor(dst, window[s][t][:].indirect(offsets_of(first, last)), gates, MULT)
+        gates_a = sbuf("gates_a", [P, PAIR], F32)
+        nc.scalar.copy(gates_a[:], gates[:, A * PAIR : (A + 1) * PAIR])
+
+        def gather(dst, s, t, first, last, factors=None):
+            if factors is None:
+                factors = gates[:, first * PAIR : last * PAIR]
+            nc.vector.tensor_tensor(dst, window[s][t][:].indirect(offsets_of(first, last)), factors, MULT)
 
         def interleave(dst, src):
             nc.scalar.copy(
@@ -113,28 +118,29 @@ def tile_moe_pre_mlp_silu_kernel(tc, xT, w1_words, w1_scales, w2_words, w2_scale
             nc.vector.quantize_mx(out=codes[:].bitcast(FP8X4), scales=scales[:], in_=src)
             return codes, scales
 
-        def first_layer(g, x_passes, h_bf, turned_tag, tag=None):
-            turned = bank(f"turned{g}", [P, 2, 2, C], turned_tag)
-            for i in range(2):
-                a = bank(f"a{g}{i}", [C, H], f"a{i}")
-                for s, (codes, scales, first) in enumerate(x_passes):
+        def first_layer(g, x_passes, h_bf, sum_tags, turned_tag, tag=None):
+            sums = [bank(f"a{g}{i}", [C, H], sum_tags[i]) for i in range(2)]
+            for s, (codes, scales, first) in enumerate(x_passes):
+                for i in range(2):
                     slots = slice(first + i * C, first + (i + 1) * C)
                     nc.tensor.matmul_mx(
-                        out=a[:],
+                        out=sums[i][:],
                         lhsT=codes[:, slots].bitcast(FP8X4),
                         lhsT_scale=scales[:, slots],
                         rhs=words1[g][:, i * PASSES + s, :].bitcast(FP4X4),
-                        rhs_scale=plane1[:, (2 * g + i) * PASSES + s, :],
+                        rhs_scale=plane1[g][:, i * PASSES + s, :],
                         start=(s == 0),
                         stop=(s == PASSES - 1),
                     )
-                h_rows = sbuf(f"h_rows{g}{i}", [C, H], BF16)
+            turned = bank(f"turned{g}", [P, 2, 2, C], turned_tag)
+            for i in range(2):
+                h_rows = sbuf(f"h_rows{g}{i}", [C, H], BF16)[:]
                 nc.scalar.activation(
-                    h_rows[:].rearrange("m (u p d) -> m u p d", u=2, d=2),
-                    a[:].rearrange("m (p u d) -> m u p d", u=2, d=2),
+                    h_rows.rearrange("m (u p d) -> m u p d", u=2, d=2),
+                    sums[i][:].rearrange("m (p u d) -> m u p d", u=2, d=2),
                     SILU,
                 )
-                pairs = h_rows[:].bitcast(F32)
+                pairs = h_rows.bitcast(F32)
                 for u in range(2):
                     nc.tensor.transpose(turned[:, i, u, :], pairs[:, u * P : (u + 1) * P], identity[:])
             nc.scalar.copy(
@@ -143,9 +149,8 @@ def tile_moe_pre_mlp_silu_kernel(tc, xT, w1_words, w1_scales, w2_words, w2_scale
             )
             return quantize(f"h{g}", h_bf, PAIR, tag)
 
-        def second_layer(g, j, h, bank_tag):
+        def second_layer(g, j, h, y_bank):
             codes, scales = h
-            y_bank = bank(f"y_bank{g}{j}", [P, PAIR], bank_tag)
             for i in range(2):
                 slots = slice(i * C, (i + 1) * C)
                 nc.tensor.matmul_mx(
@@ -157,62 +162,81 @@ def tile_moe_pre_mlp_silu_kernel(tc, xT, w1_words, w1_scales, w2_words, w2_scale
                     start=True,
                     stop=True,
                 )
-            return y_bank
 
-        def scatter(g, j, y):
-            nc.vector.tensor_copy(result[j][:].indirect(offsets_of(g, g + 1)), y)
+        def to_sbuf(name, y_bank, width, tag=None):
+            y = sbuf(name, [P, width], F32, tag)
+            nc.scalar.copy(y[:], y_bank[:])
+            return y
 
-        gathered_ab = [sbuf(f"gathered_ab{s}", [P, PACK, 2 * PAIR], F32) for s in range(PASSES)]
-        for t in range(PACK):
-            gather(gathered_ab[0][:, t, :], 0, t, A, D, gates_ab)
-        x_bf_ab0 = sbuf("x_bf_ab0", [P, 2 * PAIR * PACK], BF16)
-        interleave(x_bf_ab0[:], gathered_ab[0][:])
-        x_ab0 = quantize("x_ab0", x_bf_ab0[:], 2 * PAIR)
+        def scatter(j, first, last, y):
+            nc.vector.tensor_copy(result[j][:].indirect(offsets_of(first, last)), y[:])
+
+        def store(j):
+            nc.sync.dma_start(out[j * P : (j + 1) * P, :], result[j][:])
+
+        gathered0 = sbuf("gathered0", [P, PACK, SLOTS], F32)
+        gather(gathered0[:, 0, 0:PAIR], 0, 0, B, B + 1)
+        gather(gathered0[:, 0, PAIR:SLOTS], 0, 0, D, A + 1)
+        for t in range(1, PACK):
+            gather(gathered0[:, t, :], 0, t, B, A + 1)
+        x_bf_a0 = sbuf("x_bf_a0", [P, PAIR * PACK], BF16)
+        interleave(x_bf_a0[:], gathered0[:, :, A * PAIR : (A + 1) * PAIR])
+        x_bf_bd0 = sbuf("x_bf_bd0", [P, 2 * PAIR * PACK], BF16)
+        interleave(x_bf_bd0[:], gathered0[:, :, B * PAIR : (D + 1) * PAIR])
+
+        gathered_a1 = sbuf("gathered_a1", [P, PACK, PAIR], F32)
         for t in range(PACK - 1):
-            gather(gathered_ab[1][:, t, :], 1, t, A, D, gates_ab)
-        for g in (A, B):
-            cols = slice(g * PAIR, (g + 1) * PAIR)
-            gather(gathered_ab[1][:, PACK - 1, cols], 1, PACK - 1, g, g + 1, gates_ab[:, cols])
-
-        interleave(x_bf_a1, gathered_ab[1][:, :, 0:PAIR])
+            gather(gathered_a1[:, t, :], 1, t, A, A + 1, gates_a[:])
+        x_a0 = quantize("x_a0", x_bf_a0[:], PAIR, "gates_a")
+        gather(gathered_a1[:, PACK - 1, :], 1, PACK - 1, A, A + 1)
+        interleave(x_bf_a1, gathered_a1[:])
         x_a1 = quantize("x_a1", x_bf_a1, PAIR)
-        interleave(x_bf_b1, gathered_ab[1][:, :, PAIR : 2 * PAIR])
-        x_b1 = quantize("x_b1", x_bf_b1, PAIR)
+        x_bd0 = quantize("x_bd0", x_bf_bd0[:], 2 * PAIR, "gathered_a1")
 
-        h_a = first_layer(A, [(*x_ab0, 0), (*x_a1, 0)], h_bf_a, "bank2", "h_codes_a")
-        banks_a = [second_layer(A, j, h_a, tag) for j, tag in enumerate(("bank5", "bank7", "bank6"))]
-        y_early = sbuf("y_early", [P, 2, PAIR], F32)
-        for j in range(2):
-            nc.scalar.copy(y_early[:, j, :], banks_a[j][:])
+        h_a = first_layer(A, [(*x_a0, 0), (*x_a1, 0)], h_bf_a, ("bank0", "bank1"), "bank2", "h_codes_a")
+        banks_a = [bank(f"y_bank_a{j}", [P, PAIR], f"bank{5 + j}") for j in range(N_TILES)]
+        for j in range(N_TILES):
+            second_layer(A, j, h_a, banks_a[j][:])
+        y_a0 = to_sbuf("y_a0", banks_a[0], PAIR)
+
+        gather(gathered_bd1[:, PACK - 1, 0:PAIR], 1, PACK - 1, B, B + 1)
+        for t in range(PACK - 1):
+            gather(gathered_bd1[:, t, :], 1, t, B, D + 1)
+        x_bf_b1 = sbuf("x_bf_b1", [P, PAIR * PACK], BF16, f"h_rows{A}1")
+        interleave(x_bf_b1[:], gathered_bd1[:, :, 0:PAIR])
+        x_b1 = quantize("x_b1", x_bf_b1[:], PAIR)
+        gather(gathered_bd1[:, PACK - 1, PAIR : 2 * PAIR], 1, PACK - 1, D, D + 1)
+        x_bf_d1 = sbuf("x_bf_d1", [P, PAIR * PACK], BF16, "h_codes_a")
+        interleave(x_bf_d1[:], gathered_bd1[:, :, PAIR : 2 * PAIR])
+        x_d1 = quantize("x_d1", x_bf_d1[:], PAIR)
+        y_a1 = to_sbuf("y_a1", banks_a[1], PAIR, "shared")
 
         h_bf_b = sbuf("h_bf_b", [P, PAIR * PACK], BF16)
-        h_b = first_layer(B, [(*x_ab0, PAIR), (*x_b1, 0)], h_bf_b[:], "bank3")
-
-        x_bf_d = sbuf("x_bf_d", [P, PASSES, PAIR * PACK], BF16, "h_codes_a")
-        for s in range(PASSES):
-            for t in range(PACK):
-                gather(gathered_d[s][:, t, :], s, t, D, D + 1, gates_d[:])
-            interleave(x_bf_d[:, s, :], gathered_d[s])
-        x_d = quantize("x_d", x_bf_d[:].rearrange("p s n -> p (s n)"), PASSES * PAIR)
-
-        y_middle = sbuf("y_middle", [P, 3, PAIR], F32, "shared1")
-        nc.scalar.copy(y_middle[:, 0, :], banks_a[2][:])
-        for j, tag in enumerate(("bank2", "bank5")):
-            nc.scalar.copy(y_middle[:, 1 + j, :], second_layer(B, j, h_b, tag)[:])
+        h_b = first_layer(B, [(*x_bd0, 0), (*x_b1, 0)], h_bf_b[:], ("bank0", "bank1"), "bank3")
+        y_a2 = to_sbuf("y_a2", banks_a[2], PAIR, f"h_rows{B}1")
+        bank_b0 = bank("y_bank_b0", [P, PAIR], "bank5")
+        second_layer(B, 0, h_b, bank_b0[:])
+        banks_bd = [bank(f"y_bank_bd{j}", [P, 2 * PAIR], tag) for j, tag in ((1, "bank1"), (2, "bank6"))]
+        for j in (1, 2):
+            second_layer(B, j, h_b, banks_bd[j - 1][:, 0:PAIR])
 
         h_bf_d = sbuf("h_bf_d", [P, PAIR * PACK], BF16)
-        h_d = first_layer(D, [(*x_d, 0), (*x_d, PAIR)], h_bf_d[:], "bank4")
-        y_late = sbuf("y_late", [P, 4, PAIR], F32)
-        nc.scalar.copy(y_late[:, 0, :], second_layer(B, 2, h_b, "bank4")[:])
-        for j, tag in enumerate(("bank3", "bank7", "bank6")):
-            nc.scalar.copy(y_late[:, 1 + j, :], second_layer(D, j, h_d, tag)[:])
+        h_d = first_layer(D, [(*x_bd0, PAIR), (*x_d1, 0)], h_bf_d[:], ("bank2", "bank4"), "bank0")
+        y_b0 = to_sbuf("y_b0", bank_b0, PAIR, f"h_rows{D}1")
+        y_bd = []
+        for j in (1, 2):
+            second_layer(D, j, h_d, banks_bd[j - 1][:, PAIR : 2 * PAIR])
+            y_bd.append(to_sbuf(f"y_bd{j}", banks_bd[j - 1], 2 * PAIR))
+        bank_d0 = bank("y_bank_d0", [P, PAIR], "bank3")
+        second_layer(D, 0, h_d, bank_d0[:])
+        y_d0 = to_sbuf("y_d0", bank_d0, PAIR)
 
-        scatter(A, 0, y_early[:, 0, :])
-        scatter(A, 1, y_early[:, 1, :])
-        scatter(A, 2, y_middle[:, 0, :])
-        scatter(B, 0, y_middle[:, 1, :])
-        scatter(B, 1, y_middle[:, 2, :])
-        scatter(B, 2, y_late[:, 0, :])
-        for j in range(N_TILES):
-            scatter(D, j, y_late[:, 1 + j, :])
-            nc.sync.dma_start(out[j * P : (j + 1) * P, :], result[j][:])
+        scatter(0, A, A + 1, y_a0)
+        scatter(1, A, A + 1, y_a1)
+        scatter(2, A, A + 1, y_a2)
+        scatter(0, B, B + 1, y_b0)
+        for j in (1, 2):
+            scatter(j, B, D + 1, y_bd[j - 1])
+            store(j)
+        scatter(0, D, D + 1, y_d0)
+        store(0)

@@ -5,8 +5,19 @@ from concourse.masks import make_identity
 
 K, T, E, C, H, N = 1024, 1024, 6, 128, 512, 384
 SLOTS = E * C
+P = 128
+PACK = 4
+PASSES = K // (P * PACK)
+N_TILES = N // P
+BLOCK = 32
+LINE = 4
+PAIR = 2 * C
+
+SECOND, THIRD, FIRST = 0, 1, 2
+
 FLOPS = 2 * SLOTS * (K * H + H * N)
-BYTES = 4 * K * T + E * (K * H + H * N) // 2 + E * (K * H + H * N) // 32 + 4 * SLOTS + 2 * 128 * SLOTS // 16 + 4 * N * T
+WEIGHTS = E * (K * H + H * N)
+BYTES = 4 * K * T + WEIGHTS // 2 + WEIGHTS // BLOCK + 4 * SLOTS + 2 * P * SLOTS // 16 + 4 * N * T
 
 F32 = mybir.dt.float32
 BF16 = mybir.dt.bfloat16
@@ -19,15 +30,10 @@ FP4X4 = mybir.dt.float4_e2m1fn_x4
 SILU = mybir.ActivationFunctionType.Silu
 MULT = mybir.AluOpType.mult
 
-P = 128
-PACK = 4
-PASSES = K // (P * PACK)
-N_TILES = N // P
-PAIR = 2 * C
-B, D, A = 0, 1, 2
 
-
-def tile_moe_pre_mlp_silu_kernel(tc, xT, w1_words, w1_scales, w2_words, w2_scales, gate, offs, out):
+def tile_moe_pre_mlp_silu_kernel(
+    tc, xT, w1_words, w1_scales, w2_words, w2_scales, gate, offs, out
+):
     nc = tc.nc
     with ExitStack() as ctx:
         held = ctx.enter_context(tc.tile_pool(name="held", bufs=1))
@@ -36,23 +42,26 @@ def tile_moe_pre_mlp_silu_kernel(tc, xT, w1_words, w1_scales, w2_words, w2_scale
         def sbuf(name, shape, dtype, tag=None):
             return held.tile(shape, dtype, name=name, tag=tag or name, align_bytes=64)
 
-        def bank(name, shape, tag):
-            return psum.tile(shape, F32, name=name, tag=tag)
+        def bank(name, shape, number):
+            return psum.tile(shape, F32, name=name, tag=f"bank{number}")
+
+        def slots_of(first, last):
+            return slice(first * PAIR, (last + 1) * PAIR)
 
         offsets = held.tile([P, SLOTS // 16], U16, name="offsets")
 
         def offsets_of(first, last):
-            return offsets[:, first * PAIR // 16 : last * PAIR // 16]
+            return offsets[:, first * PAIR // 16 : (last + 1) * PAIR // 16]
 
-        plane1_bd = sbuf("plane1_bd", [P, 4 * PASSES, H], U8)
-        plane1_a = sbuf("plane1_a", [P, 2 * PASSES, H], U8)
-        plane1 = [plane1_bd[:, 0 : 2 * PASSES], plane1_bd[:, 2 * PASSES : 4 * PASSES], plane1_a[:]]
+        plane1_later = sbuf("plane1_later", [P, 4 * PASSES, H], U8)
+        plane1_first = sbuf("plane1_first", [P, 2 * PASSES, H], U8)
+        plane1 = [plane1_later[:, 0 : 2 * PASSES], plane1_later[:, 2 * PASSES : 4 * PASSES], plane1_first[:]]
         plane2 = sbuf("plane2", [P, E, N], U8)
+
         result = [sbuf(f"result{j}", [P, T], F32) for j in range(N_TILES)]
-        nc.gpsimd.memset(result[0][:], 0.0)
-        nc.gpsimd.memset(plane1_a[:].bitcast(I32), 0)
-        nc.gpsimd.memset(plane1_bd[:].bitcast(I32), 0)
-        nc.gpsimd.memset(plane2[:].bitcast(I32), 0)
+        nc.vector.memset(result[0][:], 0.0)
+        for plane in (plane1_first, plane1_later, plane2):
+            nc.gpsimd.memset(plane[:].bitcast(I32), 0)
         nc.scalar.activation(result[1][:], result[0][:], SILU)
         nc.scalar.copy(result[2][:], result[0][:])
         identity = sbuf("identity", [P, P], F32)
@@ -60,105 +69,116 @@ def tile_moe_pre_mlp_silu_kernel(tc, xT, w1_words, w1_scales, w2_words, w2_scale
 
         x_rows = xT.rearrange("(s p t) n -> s t p n", p=P, t=PACK)
         window = [[sbuf(f"window{s}{t}", [P, T], F32) for t in range(PACK)] for s in range(PASSES)]
-        words1 = [sbuf(f"words1_{g}", [P, 2 * PASSES, 2 * H], U8) for g in range(3)]
-        words2 = [sbuf(f"words2_{g}", [P, 2, 2 * N], U8) for g in range(3)]
+        words1 = [sbuf(f"words1_{g}", [P, 2 * PASSES, 2 * H], U8) for g in range(E // 2)]
+        words2 = [sbuf(f"words2_{g}", [P, 2, 2 * N], U8) for g in range(E // 2)]
 
-        shared = sbuf("shared", [P, 11 * PAIR], F32)
-        gates = shared[:, 0 : 3 * PAIR]
-        gathered_bd1 = shared[:, 2 * PAIR : 10 * PAIR].rearrange("p (t n) -> p t n", t=PACK)
-        x_bf_a1 = shared[:, 5 * PAIR : 7 * PAIR].bitcast(BF16)
-        h_bf_a = shared[:, 9 * PAIR : 11 * PAIR].bitcast(BF16)
+        reused = sbuf("reused", [P, 11 * PAIR], F32)
+        gates = reused[:, 0:SLOTS]
+        gathered_later = reused[:, 2 * PAIR : 10 * PAIR].rearrange("p (t n) -> p t n", t=PACK)
+        x_bf_first1 = [
+            reused[:, 8 * PAIR : 9 * PAIR].bitcast(BF16),
+            reused[:, 11 * PAIR // 2 : 13 * PAIR // 2].bitcast(BF16),
+        ]
+        h_bf_first = reused[:, 9 * PAIR : 11 * PAIR].bitcast(BF16)
+        reused_first = sbuf("reused_first", [P, 6 * PAIR], F32)
+        x_bf_later0 = reused_first[:, 0 : 4 * PAIR].bitcast(BF16)
+        gathered_first1 = reused_first[:, 2 * PAIR : 6 * PAIR].rearrange("p (t n) -> p t n", t=PACK)
 
         def load_window(s, t):
             nc.sync.dma_start(window[s][t][:], x_rows[s, t])
 
+        def load_gates(first, last):
+            nc.sync.dma_start(gates[:, slots_of(first, last)], gate[0:P, slots_of(first, last)])
+
         def load_words(tiles, words, g):
             nc.sync.dma_start(tiles[g][:], words[2 * g : 2 * g + 2].rearrange("e s p b -> p (e s) b"))
 
-        def load_plane(plane, scales):
-            rows = scales.rearrange("e s (q r) i -> r q (e s) i", r=4)
+        def load_plane(plane, scale_rows):
+            rows = scale_rows.rearrange("e s (q r) i -> r q (e s) i", r=4)
             for r in range(4):
                 nc.sync.dma_start(plane[:].bitcast(I32)[r:P:32], rows[r].bitcast(I32))
 
         load_window(0, 0)
-        nc.sync.dma_start(gates[:, 0:PAIR], gate[0:P, 0:PAIR])
+        load_gates(SECOND, SECOND)
         nc.sync.dma_start(offsets[:], offs)
-        nc.sync.dma_start(gates[:, PAIR:SLOTS], gate[0:P, PAIR:SLOTS])
+        load_gates(THIRD, FIRST)
         for s in range(PASSES):
             for t in range(PACK):
                 if (s, t) != (0, 0):
                     load_window(s, t)
-        load_plane(plane1_a, w1_scales[2 * A : 2 * A + 2])
-        load_words(words1, w1_words, A)
+        load_plane(plane1_first, w1_scales[2 * FIRST : 2 * FIRST + 2])
+        load_words(words1, w1_words, FIRST)
         load_plane(plane2, w2_scales)
-        load_words(words2, w2_words, A)
-        load_plane(plane1_bd, w1_scales[2 * B : 2 * D + 2])
-        load_words(words1, w1_words, B)
-        load_words(words2, w2_words, B)
-        load_words(words1, w1_words, D)
-        load_words(words2, w2_words, D)
+        load_words(words2, w2_words, FIRST)
+        load_plane(plane1_later, w1_scales[2 * SECOND : 2 * THIRD + 2])
+        for g in (SECOND, THIRD):
+            load_words(words1, w1_words, g)
+            load_words(words2, w2_words, g)
 
-        gates_a = sbuf("gates_a", [P, PAIR], F32)
-        nc.scalar.copy(gates_a[:], gates[:, A * PAIR : (A + 1) * PAIR])
+        gates_first = sbuf("gates_first", [P, PAIR], F32)
+        nc.scalar.copy(gates_first[:], gates[:, slots_of(FIRST, FIRST)])
 
-        def gather(dst, s, t, first, last, factors=None):
-            if factors is None:
-                factors = gates[:, first * PAIR : last * PAIR]
+        def gather(dst, s, t, first, last, factors):
             nc.vector.tensor_tensor(dst, window[s][t][:].indirect(offsets_of(first, last)), factors, MULT)
 
         def interleave(dst, src):
             nc.scalar.copy(
-                dst.rearrange("p (c i t) -> p c t i", i=4, t=PACK),
-                src.rearrange("p t (c i) -> p c t i", i=4),
+                dst.rearrange("p (c i t) -> p c t i", i=LINE, t=PACK),
+                src.rearrange("p t (c i) -> p c t i", i=LINE),
             )
 
-        def quantize(name, src, words, tag=None):
-            codes = sbuf(f"{name}_codes", [P, words], U32, tag)
-            scales = sbuf(f"{name}_scales", [P, words], U8)
+        def quantize(name, src, width, tag=None):
+            codes = sbuf(f"{name}_codes", [P, width], U32, tag)
+            scales = sbuf(f"{name}_scales", [P, width], U8)
             nc.vector.quantize_mx(out=codes[:].bitcast(FP8X4), scales=scales[:], in_=src)
             return codes, scales
 
-        def first_layer(g, x_passes, h_bf, sum_tags, turned_tag, tag=None):
-            sums = [bank(f"a{g}{i}", [C, H], sum_tags[i]) for i in range(2)]
-            for s, (codes, scales, first) in enumerate(x_passes):
-                for i in range(2):
-                    slots = slice(first + i * C, first + (i + 1) * C)
+        def expert_of(quantized, column):
+            codes, scales = quantized
+            return codes[:, column : column + C].bitcast(FP8X4), scales[:, column : column + C]
+
+        def experts_of(quantized, column):
+            return [expert_of(quantized, column + e * C) for e in range(2)]
+
+        def first_layer(g, x_passes, sum_banks, turned_bank, h_bf, rows_tag, codes_tag=None):
+            sums = [bank(f"sums{g}{e}", [C, H], sum_banks[e]) for e in range(2)]
+            for s in range(PASSES):
+                for e in range(2):
+                    codes, scales = x_passes[s][e]
                     nc.tensor.matmul_mx(
-                        out=sums[i][:],
-                        lhsT=codes[:, slots].bitcast(FP8X4),
-                        lhsT_scale=scales[:, slots],
-                        rhs=words1[g][:, i * PASSES + s, :].bitcast(FP4X4),
-                        rhs_scale=plane1[g][:, i * PASSES + s, :],
+                        out=sums[e][:],
+                        lhsT=codes,
+                        lhsT_scale=scales,
+                        rhs=words1[g][:, e * PASSES + s, :].bitcast(FP4X4),
+                        rhs_scale=plane1[g][:, e * PASSES + s, :],
                         start=(s == 0),
                         stop=(s == PASSES - 1),
                     )
-            turned = bank(f"turned{g}", [P, 2, 2, C], turned_tag)
-            for i in range(2):
-                h_rows = sbuf(f"h_rows{g}{i}", [C, H], BF16)[:]
+            turned = bank(f"turned{g}", [P, 2, 2, C], turned_bank)
+            h_rows = sbuf(f"h_rows{g}", [C, 2, H], BF16, rows_tag)
+            for e in range(2):
                 nc.scalar.activation(
-                    h_rows.rearrange("m (u p d) -> m u p d", u=2, d=2),
-                    sums[i][:].rearrange("m (p u d) -> m u p d", u=2, d=2),
+                    h_rows[:, e, :].rearrange("m (u p d) -> m u p d", u=2, d=2),
+                    sums[e][:].rearrange("m (p u d) -> m u p d", u=2, d=2),
                     SILU,
                 )
-                pairs = h_rows.bitcast(F32)
+                h_words = h_rows[:, e, :].bitcast(F32)
                 for u in range(2):
-                    nc.tensor.transpose(turned[:, i, u, :], pairs[:, u * P : (u + 1) * P], identity[:])
+                    nc.tensor.transpose(turned[:, e, u, :], h_words[:, u * P : (u + 1) * P], identity[:])
             nc.scalar.copy(
                 h_bf.bitcast(F32).rearrange("p (e c u) -> p e c u", c=C, u=2),
                 turned[:].rearrange("p e u c -> p e c u"),
             )
-            return quantize(f"h{g}", h_bf, PAIR, tag)
+            return quantize(f"h{g}", h_bf, PAIR, codes_tag)
 
         def second_layer(g, j, h, y_bank):
-            codes, scales = h
-            for i in range(2):
-                slots = slice(i * C, (i + 1) * C)
+            for e, (codes, scales) in enumerate(experts_of(h, 0)):
                 nc.tensor.matmul_mx(
-                    out=y_bank[:, slots],
-                    lhsT=words2[g][:, i, 2 * P * j : 2 * P * (j + 1)].bitcast(FP4X4),
-                    lhsT_scale=plane2[:, 2 * g + i, P * j : P * (j + 1)],
-                    rhs=codes[:, slots].bitcast(FP8X4),
-                    rhs_scale=scales[:, slots],
+                    out=y_bank[:, e * C : (e + 1) * C],
+                    lhsT=words2[g][:, e, 2 * P * j : 2 * P * (j + 1)].bitcast(FP4X4),
+                    lhsT_scale=plane2[:, 2 * g + e, P * j : P * (j + 1)],
+                    rhs=codes,
+                    rhs_scale=scales,
                     start=True,
                     stop=True,
                 )
@@ -175,68 +195,81 @@ def tile_moe_pre_mlp_silu_kernel(tc, xT, w1_words, w1_scales, w2_words, w2_scale
             nc.sync.dma_start(out[j * P : (j + 1) * P, :], result[j][:])
 
         gathered0 = sbuf("gathered0", [P, PACK, SLOTS], F32)
-        gather(gathered0[:, 0, 0:PAIR], 0, 0, B, B + 1)
-        gather(gathered0[:, 0, PAIR:SLOTS], 0, 0, D, A + 1)
+        for first, last in ((SECOND, SECOND), (THIRD, FIRST)):
+            gather(gathered0[:, 0, slots_of(first, last)], 0, 0, first, last, gates[:, slots_of(first, last)])
         for t in range(1, PACK):
-            gather(gathered0[:, t, :], 0, t, B, A + 1)
-        x_bf_a0 = sbuf("x_bf_a0", [P, PAIR * PACK], BF16)
-        interleave(x_bf_a0[:], gathered0[:, :, A * PAIR : (A + 1) * PAIR])
-        x_bf_bd0 = sbuf("x_bf_bd0", [P, 2 * PAIR * PACK], BF16)
-        interleave(x_bf_bd0[:], gathered0[:, :, B * PAIR : (D + 1) * PAIR])
+            gather(gathered0[:, t, :], 0, t, SECOND, FIRST, gates)
+        x_bf_first0 = sbuf("x_bf_first0", [P, PAIR * PACK], BF16)
+        interleave(x_bf_first0[:], gathered0[:, :, slots_of(FIRST, FIRST)])
+        interleave(x_bf_later0[:, 0 : PAIR * PACK], gathered0[:, :, slots_of(SECOND, SECOND)])
 
-        gathered_a1 = sbuf("gathered_a1", [P, PACK, PAIR], F32)
         for t in range(PACK - 1):
-            gather(gathered_a1[:, t, :], 1, t, A, A + 1, gates_a[:])
-        x_a0 = quantize("x_a0", x_bf_a0[:], PAIR, "gates_a")
-        gather(gathered_a1[:, PACK - 1, :], 1, PACK - 1, A, A + 1)
-        interleave(x_bf_a1, gathered_a1[:])
-        x_a1 = quantize("x_a1", x_bf_a1, PAIR)
-        x_bd0 = quantize("x_bd0", x_bf_bd0[:], 2 * PAIR, "gathered_a1")
+            gather(gathered_first1[:, t, :], 1, t, FIRST, FIRST, gates_first[:])
+        x_first0 = quantize("x_first0", x_bf_first0[:], PAIR, "gates_first")
+        gather(gathered_first1[:, PACK - 1, :], 1, PACK - 1, FIRST, FIRST, gates[:, slots_of(FIRST, FIRST)])
+        x_first1 = []
+        for e in range(2):
+            interleave(x_bf_first1[e], gathered_first1[:, :, e * C : (e + 1) * C])
+            x_first1.append(expert_of(quantize(f"x_first1{e}", x_bf_first1[e], C), 0))
+        interleave(x_bf_later0[:, PAIR * PACK : 2 * PAIR * PACK], gathered0[:, :, slots_of(THIRD, THIRD)])
+        x_later0 = quantize("x_later0", x_bf_later0, 2 * PAIR)
 
-        h_a = first_layer(A, [(*x_a0, 0), (*x_a1, 0)], h_bf_a, ("bank0", "bank1"), "bank2", "h_codes_a")
-        banks_a = [bank(f"y_bank_a{j}", [P, PAIR], f"bank{5 + j}") for j in range(N_TILES)]
+        h_first = first_layer(
+            FIRST, [experts_of(x_first0, 0), x_first1], (0, 1), 2, h_bf_first, "h_rows_first", "h_codes_first"
+        )
+        banks_first = [bank(f"y_bank_first{j}", [P, PAIR], 5 + j) for j in range(N_TILES)]
         for j in range(N_TILES):
-            second_layer(A, j, h_a, banks_a[j][:])
-        y_a0 = to_sbuf("y_a0", banks_a[0], PAIR)
+            second_layer(FIRST, j, h_first, banks_first[j][:])
+        y_first0 = to_sbuf("y_first0", banks_first[0], PAIR)
 
-        gather(gathered_bd1[:, PACK - 1, 0:PAIR], 1, PACK - 1, B, B + 1)
-        for t in range(PACK - 1):
-            gather(gathered_bd1[:, t, :], 1, t, B, D + 1)
-        x_bf_b1 = sbuf("x_bf_b1", [P, PAIR * PACK], BF16, f"h_rows{A}1")
-        interleave(x_bf_b1[:], gathered_bd1[:, :, 0:PAIR])
-        x_b1 = quantize("x_b1", x_bf_b1[:], PAIR)
-        gather(gathered_bd1[:, PACK - 1, PAIR : 2 * PAIR], 1, PACK - 1, D, D + 1)
-        x_bf_d1 = sbuf("x_bf_d1", [P, PAIR * PACK], BF16, "h_codes_a")
-        interleave(x_bf_d1[:], gathered_bd1[:, :, PAIR : 2 * PAIR])
-        x_d1 = quantize("x_d1", x_bf_d1[:], PAIR)
-        y_a1 = to_sbuf("y_a1", banks_a[1], PAIR, "shared")
+        gates_later = gates[:, slots_of(SECOND, THIRD)]
+        gather(gathered_later[:, 0, :], 1, 0, SECOND, THIRD, gates_later)
+        gather(gathered_later[:, PACK - 1, 0:PAIR], 1, PACK - 1, SECOND, SECOND, gates_later[:, 0:PAIR])
+        for t in range(1, PACK - 1):
+            gather(gathered_later[:, t, :], 1, t, SECOND, THIRD, gates_later)
+        x_bf_second1 = sbuf("x_bf_second1", [P, PAIR * PACK], BF16, "h_rows_first")
+        interleave(x_bf_second1[:], gathered_later[:, :, 0:PAIR])
+        x_second1 = quantize("x_second1", x_bf_second1[:], PAIR)
+        gather(
+            gathered_later[:, PACK - 1, PAIR : 2 * PAIR], 1, PACK - 1, THIRD, THIRD, gates_later[:, PAIR : 2 * PAIR]
+        )
+        x_bf_third1 = sbuf("x_bf_third1", [P, PAIR * PACK], BF16, "h_codes_first")
+        interleave(x_bf_third1[:], gathered_later[:, :, PAIR : 2 * PAIR])
+        x_third1 = quantize("x_third1", x_bf_third1[:], PAIR)
+        y_first1 = to_sbuf("y_first1", banks_first[1], PAIR, "reused")
 
-        h_bf_b = sbuf("h_bf_b", [P, PAIR * PACK], BF16)
-        h_b = first_layer(B, [(*x_bd0, 0), (*x_b1, 0)], h_bf_b[:], ("bank0", "bank1"), "bank3")
-        y_a2 = to_sbuf("y_a2", banks_a[2], PAIR, f"h_rows{B}1")
-        bank_b0 = bank("y_bank_b0", [P, PAIR], "bank5")
-        second_layer(B, 0, h_b, bank_b0[:])
-        banks_bd = [bank(f"y_bank_bd{j}", [P, 2 * PAIR], tag) for j, tag in ((1, "bank1"), (2, "bank6"))]
-        for j in (1, 2):
-            second_layer(B, j, h_b, banks_bd[j - 1][:, 0:PAIR])
+        h_bf_second = sbuf("h_bf_second", [P, PAIR * PACK], BF16)
+        h_second = first_layer(
+            SECOND, [experts_of(x_later0, 0), experts_of(x_second1, 0)], (0, 1), 3, h_bf_second[:], "h_rows_second"
+        )
+        y_first2 = to_sbuf("y_first2", banks_first[2], PAIR, "h_rows_second")
+        bank_second0 = bank("y_bank_second0", [P, PAIR], 2)
+        second_layer(SECOND, 0, h_second, bank_second0[:])
+        y_second0 = to_sbuf("y_second0", bank_second0, PAIR)
+        bank_second1 = bank("y_bank_second1", [P, PAIR], 5)
+        second_layer(SECOND, 1, h_second, bank_second1[:])
+        bank_later2 = bank("y_bank_later2", [P, 2 * PAIR], 4)
+        second_layer(SECOND, 2, h_second, bank_later2[:, 0:PAIR])
 
-        h_bf_d = sbuf("h_bf_d", [P, PAIR * PACK], BF16)
-        h_d = first_layer(D, [(*x_bd0, PAIR), (*x_d1, 0)], h_bf_d[:], ("bank2", "bank4"), "bank0")
-        y_b0 = to_sbuf("y_b0", bank_b0, PAIR, f"h_rows{D}1")
-        y_bd = []
-        for j in (1, 2):
-            second_layer(D, j, h_d, banks_bd[j - 1][:, PAIR : 2 * PAIR])
-            y_bd.append(to_sbuf(f"y_bd{j}", banks_bd[j - 1], 2 * PAIR))
-        bank_d0 = bank("y_bank_d0", [P, PAIR], "bank3")
-        second_layer(D, 0, h_d, bank_d0[:])
-        y_d0 = to_sbuf("y_d0", bank_d0, PAIR)
+        h_bf_third = sbuf("h_bf_third", [P, PAIR * PACK], BF16)
+        h_third = first_layer(
+            THIRD, [experts_of(x_later0, PAIR), experts_of(x_third1, 0)], (1, 3), 0, h_bf_third[:], "h_bf_second"
+        )
+        y_second1 = to_sbuf("y_second1", bank_second1, PAIR, "h_bf_second")
+        second_layer(THIRD, 2, h_third, bank_later2[:, PAIR : 2 * PAIR])
+        y_later2 = to_sbuf("y_later2", bank_later2, 2 * PAIR)
+        y_third = []
+        for j in range(2):
+            bank_third = bank(f"y_bank_third{j}", [P, PAIR], 6 + j)
+            second_layer(THIRD, j, h_third, bank_third[:])
+            y_third.append(to_sbuf(f"y_third{j}", bank_third, PAIR))
 
-        scatter(0, A, A + 1, y_a0)
-        scatter(1, A, A + 1, y_a1)
-        scatter(2, A, A + 1, y_a2)
-        scatter(0, B, B + 1, y_b0)
-        for j in (1, 2):
-            scatter(j, B, D + 1, y_bd[j - 1])
+        for j, y in enumerate((y_first0, y_first1, y_first2)):
+            scatter(j, FIRST, FIRST, y)
+        for j, y in enumerate((y_second0, y_second1)):
+            scatter(j, SECOND, SECOND, y)
+        scatter(2, SECOND, THIRD, y_later2)
+        store(2)
+        for j, y in enumerate(y_third):
+            scatter(j, THIRD, THIRD, y)
             store(j)
-        scatter(0, D, D + 1, y_d0)
-        store(0)

from contextlib import ExitStack

import concourse.mybir as mybir
from concourse.masks import make_identity

K, T, E, C, H, N = 1024, 1024, 6, 128, 512, 384
SLOTS = E * C
P = 128
PACK = 4
PASSES = K // (P * PACK)
N_TILES = N // P
BLOCK = 32
LINE = 4
PAIR = 2 * C

SECOND, THIRD, FIRST = 0, 1, 2

FLOPS = 2 * SLOTS * (K * H + H * N)
WEIGHTS = E * (K * H + H * N)
BYTES = 4 * K * T + WEIGHTS // 2 + WEIGHTS // BLOCK + 4 * SLOTS + 2 * P * SLOTS // 16 + 4 * N * T

F32 = mybir.dt.float32
BF16 = mybir.dt.bfloat16
I32 = mybir.dt.int32
U32 = mybir.dt.uint32
U16 = mybir.dt.uint16
U8 = mybir.dt.uint8
FP8X4 = mybir.dt.float8_e4m3fn_x4
FP4X4 = mybir.dt.float4_e2m1fn_x4
SILU = mybir.ActivationFunctionType.Silu
MULT = mybir.AluOpType.mult


def tile_moe_pre_mlp_silu_kernel(
    tc, xT, w1_words, w1_scales, w2_words, w2_scales, gate, offs, out
):
    nc = tc.nc
    with ExitStack() as ctx:
        held = ctx.enter_context(tc.tile_pool(name="held", bufs=1))
        psum = ctx.enter_context(tc.psum_pool(name="psum", bufs=1))

        def sbuf(name, shape, dtype, tag=None):
            return held.tile(shape, dtype, name=name, tag=tag or name, align_bytes=64)

        def bank(name, shape, number):
            return psum.tile(shape, F32, name=name, tag=f"bank{number}")

        def slots_of(first, last):
            return slice(first * PAIR, (last + 1) * PAIR)

        offsets = held.tile([P, SLOTS // 16], U16, name="offsets")

        def offsets_of(first, last):
            return offsets[:, first * PAIR // 16 : (last + 1) * PAIR // 16]

        plane1_later = sbuf("plane1_later", [P, 4 * PASSES, H], U8)
        plane1_first = sbuf("plane1_first", [P, 2 * PASSES, H], U8)
        plane1 = [plane1_later[:, 0 : 2 * PASSES], plane1_later[:, 2 * PASSES : 4 * PASSES], plane1_first[:]]
        plane2 = sbuf("plane2", [P, E, N], U8)

        result = [sbuf(f"result{j}", [P, T], F32) for j in range(N_TILES)]
        nc.vector.memset(result[0][:], 0.0)
        for plane in (plane1_first, plane1_later, plane2):
            nc.gpsimd.memset(plane[:].bitcast(I32), 0)
        nc.scalar.activation(result[1][:], result[0][:], SILU)
        nc.scalar.copy(result[2][:], result[0][:])
        identity = sbuf("identity", [P, P], F32)
        make_identity(nc, identity[:])

        x_rows = xT.rearrange("(s p t) n -> s t p n", p=P, t=PACK)
        window = [[sbuf(f"window{s}{t}", [P, T], F32) for t in range(PACK)] for s in range(PASSES)]
        words1 = [sbuf(f"words1_{g}", [P, 2 * PASSES, 2 * H], U8) for g in range(E // 2)]
        words2 = [sbuf(f"words2_{g}", [P, 2, 2 * N], U8) for g in range(E // 2)]

        reused = sbuf("reused", [P, 11 * PAIR], F32)
        gates = reused[:, 0:SLOTS]
        gathered_later = reused[:, 2 * PAIR : 10 * PAIR].rearrange("p (t n) -> p t n", t=PACK)
        x_bf_first1 = [
            reused[:, 8 * PAIR : 9 * PAIR].bitcast(BF16),
            reused[:, 11 * PAIR // 2 : 13 * PAIR // 2].bitcast(BF16),
        ]
        h_bf_first = reused[:, 9 * PAIR : 11 * PAIR].bitcast(BF16)
        reused_first = sbuf("reused_first", [P, 6 * PAIR], F32)
        x_bf_later0 = reused_first[:, 0 : 4 * PAIR].bitcast(BF16)
        gathered_first1 = reused_first[:, 2 * PAIR : 6 * PAIR].rearrange("p (t n) -> p t n", t=PACK)

        def load_window(s, t):
            nc.sync.dma_start(window[s][t][:], x_rows[s, t])

        def load_gates(first, last):
            nc.sync.dma_start(gates[:, slots_of(first, last)], gate[0:P, slots_of(first, last)])

        def load_words(tiles, words, g):
            nc.sync.dma_start(tiles[g][:], words[2 * g : 2 * g + 2].rearrange("e s p b -> p (e s) b"))

        def load_plane(plane, scale_rows):
            rows = scale_rows.rearrange("e s (q r) i -> r q (e s) i", r=4)
            for r in range(4):
                nc.sync.dma_start(plane[:].bitcast(I32)[r:P:32], rows[r].bitcast(I32))

        load_window(0, 0)
        load_gates(SECOND, SECOND)
        nc.sync.dma_start(offsets[:], offs)
        load_gates(THIRD, FIRST)
        for s in range(PASSES):
            for t in range(PACK):
                if (s, t) != (0, 0):
                    load_window(s, t)
        load_plane(plane1_first, w1_scales[2 * FIRST : 2 * FIRST + 2])
        load_words(words1, w1_words, FIRST)
        load_plane(plane2, w2_scales)
        load_words(words2, w2_words, FIRST)
        load_plane(plane1_later, w1_scales[2 * SECOND : 2 * THIRD + 2])
        for g in (SECOND, THIRD):
            load_words(words1, w1_words, g)
            load_words(words2, w2_words, g)

        gates_first = sbuf("gates_first", [P, PAIR], F32)
        nc.scalar.copy(gates_first[:], gates[:, slots_of(FIRST, FIRST)])

        def gather(dst, s, t, first, last, factors):
            nc.vector.tensor_tensor(dst, window[s][t][:].indirect(offsets_of(first, last)), factors, MULT)

        def interleave(dst, src):
            nc.scalar.copy(
                dst.rearrange("p (c i t) -> p c t i", i=LINE, t=PACK),
                src.rearrange("p t (c i) -> p c t i", i=LINE),
            )

        def quantize(name, src, width, tag=None):
            codes = sbuf(f"{name}_codes", [P, width], U32, tag)
            scales = sbuf(f"{name}_scales", [P, width], U8)
            nc.vector.quantize_mx(out=codes[:].bitcast(FP8X4), scales=scales[:], in_=src)
            return codes, scales

        def expert_of(quantized, column):
            codes, scales = quantized
            return codes[:, column : column + C].bitcast(FP8X4), scales[:, column : column + C]

        def experts_of(quantized, column):
            return [expert_of(quantized, column + e * C) for e in range(2)]

        def first_layer(g, x_passes, sum_banks, turned_bank, h_bf, rows_tag, codes_tag=None):
            sums = [bank(f"sums{g}{e}", [C, H], sum_banks[e]) for e in range(2)]
            for s in range(PASSES):
                for e in range(2):
                    codes, scales = x_passes[s][e]
                    nc.tensor.matmul_mx(
                        out=sums[e][:],
                        lhsT=codes,
                        lhsT_scale=scales,
                        rhs=words1[g][:, e * PASSES + s, :].bitcast(FP4X4),
                        rhs_scale=plane1[g][:, e * PASSES + s, :],
                        start=(s == 0),
                        stop=(s == PASSES - 1),
                    )
            turned = bank(f"turned{g}", [P, 2, 2, C], turned_bank)
            h_rows = sbuf(f"h_rows{g}", [C, 2, H], BF16, rows_tag)
            for e in range(2):
                nc.scalar.activation(
                    h_rows[:, e, :].rearrange("m (u p d) -> m u p d", u=2, d=2),
                    sums[e][:].rearrange("m (p u d) -> m u p d", u=2, d=2),
                    SILU,
                )
                h_words = h_rows[:, e, :].bitcast(F32)
                for u in range(2):
                    nc.tensor.transpose(turned[:, e, u, :], h_words[:, u * P : (u + 1) * P], identity[:])
            nc.scalar.copy(
                h_bf.bitcast(F32).rearrange("p (e c u) -> p e c u", c=C, u=2),
                turned[:].rearrange("p e u c -> p e c u"),
            )
            return quantize(f"h{g}", h_bf, PAIR, codes_tag)

        def second_layer(g, j, h, y_bank):
            for e, (codes, scales) in enumerate(experts_of(h, 0)):
                nc.tensor.matmul_mx(
                    out=y_bank[:, e * C : (e + 1) * C],
                    lhsT=words2[g][:, e, 2 * P * j : 2 * P * (j + 1)].bitcast(FP4X4),
                    lhsT_scale=plane2[:, 2 * g + e, P * j : P * (j + 1)],
                    rhs=codes,
                    rhs_scale=scales,
                    start=True,
                    stop=True,
                )

        def to_sbuf(name, y_bank, width, tag=None):
            y = sbuf(name, [P, width], F32, tag)
            nc.scalar.copy(y[:], y_bank[:])
            return y

        def scatter(j, first, last, y):
            nc.vector.tensor_copy(result[j][:].indirect(offsets_of(first, last)), y[:])

        def store(j):
            nc.sync.dma_start(out[j * P : (j + 1) * P, :], result[j][:])

        gathered0 = sbuf("gathered0", [P, PACK, SLOTS], F32)
        for first, last in ((SECOND, SECOND), (THIRD, FIRST)):
            gather(gathered0[:, 0, slots_of(first, last)], 0, 0, first, last, gates[:, slots_of(first, last)])
        for t in range(1, PACK):
            gather(gathered0[:, t, :], 0, t, SECOND, FIRST, gates)
        x_bf_first0 = sbuf("x_bf_first0", [P, PAIR * PACK], BF16)
        interleave(x_bf_first0[:], gathered0[:, :, slots_of(FIRST, FIRST)])
        interleave(x_bf_later0[:, 0 : PAIR * PACK], gathered0[:, :, slots_of(SECOND, SECOND)])

        for t in range(PACK - 1):
            gather(gathered_first1[:, t, :], 1, t, FIRST, FIRST, gates_first[:])
        x_first0 = quantize("x_first0", x_bf_first0[:], PAIR, "gates_first")
        gather(gathered_first1[:, PACK - 1, :], 1, PACK - 1, FIRST, FIRST, gates[:, slots_of(FIRST, FIRST)])
        x_first1 = []
        for e in range(2):
            interleave(x_bf_first1[e], gathered_first1[:, :, e * C : (e + 1) * C])
            x_first1.append(expert_of(quantize(f"x_first1{e}", x_bf_first1[e], C), 0))
        interleave(x_bf_later0[:, PAIR * PACK : 2 * PAIR * PACK], gathered0[:, :, slots_of(THIRD, THIRD)])
        x_later0 = quantize("x_later0", x_bf_later0, 2 * PAIR)

        h_first = first_layer(
            FIRST, [experts_of(x_first0, 0), x_first1], (0, 1), 2, h_bf_first, "h_rows_first", "h_codes_first"
        )
        banks_first = [bank(f"y_bank_first{j}", [P, PAIR], 5 + j) for j in range(N_TILES)]
        for j in range(N_TILES):
            second_layer(FIRST, j, h_first, banks_first[j][:])
        y_first0 = to_sbuf("y_first0", banks_first[0], PAIR)

        gates_later = gates[:, slots_of(SECOND, THIRD)]
        gather(gathered_later[:, 0, :], 1, 0, SECOND, THIRD, gates_later)
        gather(gathered_later[:, PACK - 1, 0:PAIR], 1, PACK - 1, SECOND, SECOND, gates_later[:, 0:PAIR])
        for t in range(1, PACK - 1):
            gather(gathered_later[:, t, :], 1, t, SECOND, THIRD, gates_later)
        x_bf_second1 = sbuf("x_bf_second1", [P, PAIR * PACK], BF16, "h_rows_first")
        interleave(x_bf_second1[:], gathered_later[:, :, 0:PAIR])
        x_second1 = quantize("x_second1", x_bf_second1[:], PAIR)
        gather(
            gathered_later[:, PACK - 1, PAIR : 2 * PAIR], 1, PACK - 1, THIRD, THIRD, gates_later[:, PAIR : 2 * PAIR]
        )
        x_bf_third1 = sbuf("x_bf_third1", [P, PAIR * PACK], BF16, "h_codes_first")
        interleave(x_bf_third1[:], gathered_later[:, :, PAIR : 2 * PAIR])
        x_third1 = quantize("x_third1", x_bf_third1[:], PAIR)
        y_first1 = to_sbuf("y_first1", banks_first[1], PAIR, "reused")

        h_bf_second = sbuf("h_bf_second", [P, PAIR * PACK], BF16)
        h_second = first_layer(
            SECOND, [experts_of(x_later0, 0), experts_of(x_second1, 0)], (0, 1), 3, h_bf_second[:], "h_rows_second"
        )
        y_first2 = to_sbuf("y_first2", banks_first[2], PAIR, "h_rows_second")
        bank_second0 = bank("y_bank_second0", [P, PAIR], 2)
        second_layer(SECOND, 0, h_second, bank_second0[:])
        y_second0 = to_sbuf("y_second0", bank_second0, PAIR)
        bank_second1 = bank("y_bank_second1", [P, PAIR], 5)
        second_layer(SECOND, 1, h_second, bank_second1[:])
        bank_later2 = bank("y_bank_later2", [P, 2 * PAIR], 4)
        second_layer(SECOND, 2, h_second, bank_later2[:, 0:PAIR])

        h_bf_third = sbuf("h_bf_third", [P, PAIR * PACK], BF16)
        h_third = first_layer(
            THIRD, [experts_of(x_later0, PAIR), experts_of(x_third1, 0)], (1, 3), 0, h_bf_third[:], "h_bf_second"
        )
        y_second1 = to_sbuf("y_second1", bank_second1, PAIR, "h_bf_second")
        second_layer(THIRD, 2, h_third, bank_later2[:, PAIR : 2 * PAIR])
        y_later2 = to_sbuf("y_later2", bank_later2, 2 * PAIR)
        y_third = []
        for j in range(2):
            bank_third = bank(f"y_bank_third{j}", [P, PAIR], 6 + j)
            second_layer(THIRD, j, h_third, bank_third[:])
            y_third.append(to_sbuf(f"y_third{j}", bank_third, PAIR))

        for j, y in enumerate((y_first0, y_first1, y_first2)):
            scatter(j, FIRST, FIRST, y)
        for j, y in enumerate((y_second0, y_second1)):
            scatter(j, SECOND, SECOND, y)
        scatter(2, SECOND, THIRD, y_later2)
        store(2)
        for j, y in enumerate(y_third):
            scatter(j, THIRD, THIRD, y)
            store(j)
